import numpy as np
import ml_dtypes


def mxq(x, axis, fmt="e4m3"):
    dtype, down = {"e4m3": (ml_dtypes.float8_e4m3fn, 7), "e5m2": (ml_dtypes.float8_e5m2, 14)}[fmt]
    v = np.moveaxis(np.asarray(x, np.float32).astype(ml_dtypes.bfloat16).astype(np.float64), axis, -1)
    blocks = v.reshape(v.shape[:-1] + (-1, 32))
    amax = np.abs(blocks).max(-1, keepdims=True)
    byte = np.maximum(np.where(amax > 0, np.frexp(amax)[1] - 1 + 127, 0) - down, 1)
    scale = np.exp2(byte - 127.0)
    codes = (blocks / scale).astype(np.float32).astype(dtype).astype(np.float64)
    return np.moveaxis((codes * scale).reshape(v.shape), -1, axis)


WIDE = False


def mx_kscale(k):
    if not WIDE:
        return np.ones(k)
    levels = np.array([10, -10, 5, -5, 0])
    if k % 512:
        return np.exp2(np.random.permutation(np.resize(levels, k // 32))).repeat(32)
    a = np.empty((k // 512, 16))
    for p in range(k // 512):
        a[p, :8] = np.random.permutation(np.resize(levels, 8))
        for g in range(8):
            far = levels[np.abs(levels - a[p, g]) >= 10]
            a[p, g + 8] = far[np.random.randint(len(far))]
    return np.exp2(a.ravel()).repeat(32)


def f64(x):
    return np.asarray(x).astype(np.float64)


def striped(idx):
    return np.tile(idx.reshape(-1, 16).T, (8, 1)).astype(np.uint16)


def unstriped(offs):
    return offs[:16].T.reshape(-1).astype(np.int64)


def striped8(idx):
    return np.concatenate([x.reshape(-1, 16).T for x in idx]).astype(np.uint16)


def runs(offs, k):
    lists = np.stack([offs[16 * r : 16 * r + 16].T.reshape(-1) for r in range(8)]).astype(np.int64)
    return lists[np.arange(k) % 512 // 64]


def pack_weight(w):
    k, n = w.shape
    w = f64(np.asarray(w, np.float32).astype(ml_dtypes.bfloat16)).reshape(k // 32, 32, n)
    amax = np.abs(w).max(1)
    byte = np.clip(np.where(amax > 0, np.frexp(amax)[1] - 1 + 127 - 7, 1), 1, 254)
    scaled = (w * np.exp2(127.0 - byte)[:, None, :]).reshape(k, n).astype(np.float32)
    words = np.ascontiguousarray(scaled.reshape(k // 512, 128, 4, n).transpose(0, 1, 3, 2)).astype(ml_dtypes.float8_e4m3fn).view(np.uint8)
    return words, np.ascontiguousarray(byte.astype(np.uint8).reshape(k // 512, 16, n))


def unpack_weight(words, scales):
    g, p, n, _ = words.shape
    vals = np.ascontiguousarray(words).view(ml_dtypes.float8_e4m3fn).astype(np.float64) * np.repeat(np.exp2(scales.astype(np.float64) - 127.0), 8, axis=1)[..., None]
    return vals.transpose(0, 1, 3, 2).reshape(g * 512, n)


def sigmoid(v):
    return 1.0 / (1.0 + np.exp(-np.maximum(v, -700.0)))


K, T, S, N, H, G = 512, 2048, 512, 512, 512, 2048


def setup_inputs():
    n = np.random.standard_normal
    s = mx_kscale(K)[:, None]
    u = mx_kscale(H)
    packed_xT = pack_weight(n((K, T)) * s)
    packed_dT = pack_weight(n((K, G)) / s)
    return {
        "x_words": packed_xT[0],
        "x_scales": packed_xT[1],
        "w1": (n((K, H)) / np.sqrt(K) / s).astype(np.float32),
        "gs": (np.random.uniform(0.5, 1.5, (K, 1)) * s).astype(np.float32),
        "d_words": packed_dT[0],
        "d_scales": packed_dT[1],
        "gn": (np.random.uniform(0.5, 1.5, (H, 1)) * u[:, None]).astype(np.float32),
        "res": n((N, S)).astype(np.float32),
        "w2": (n((H, N)) / np.sqrt(H) / u[:, None]).astype(np.float32),
        "offs": striped(np.random.permutation(T)[:S]),
        "nb": striped8(np.stack([np.random.permutation(S) for _ in range(8)])),
        "kidx": striped8(np.random.randint(0, G, (8, H))),
    }


def reference(x_words, x_scales, w1, gs, d_words, d_scales, gn, res, w2, offs, nb, kidx):
    d_kidx = unpack_weight(d_words, d_scales)[np.arange(K)[:, None], runs(kidx, K)]
    xq = unpack_weight(x_words, x_scales)[:, unstriped(offs)]
    y = mxq(f64(w1), 0, "e4m3").T @ xq
    zq = f64(gs) * (y - (y[np.arange(H)[:, None], runs(nb, H)]))
    s = 0.0625 * ((d_kidx.T @ mxq(zq, 0, "e4m3")))
    z2 = f64(gn) * sigmoid(s)
    return f64(res) + (mxq(f64(w2), 0, "e4m3").T @ mxq(z2, 0, "e4m3"))

@@ -1,0 +1,194 @@
+from contextlib import ExitStack
+
+import concourse.mybir as mybir
+
+K, T, S, N, H, G = 512, 2048, 512, 512, 512, 2048
+FLOPS = 2 * S * (K * H + K * H + H * N)
+
+F32 = mybir.dt.float32
+BF16 = mybir.dt.bfloat16
+I32 = mybir.dt.int32
+U32 = mybir.dt.uint32
+U16 = mybir.dt.uint16
+U8 = mybir.dt.uint8
+FP8X4 = mybir.dt.float8_e4m3fn_x4
+ALU = mybir.AluOpType
+ACT = mybir.ActivationFunctionType
+
+P = 128
+PACK = 4
+LIST_ROWS = 16
+UNIT = 128
+GATHERS = ((0, 256), (256, 512))
+
+
+def tile_picked_pqhop_sigmoid_p_kernel(tc, x_words, x_scales, w1, gs, d_words, d_scales, gn, res, w2, offs, nb, kidx, out):
+    nc = tc.nc
+    with ExitStack() as ctx:
+        lists = ctx.enter_context(tc.tile_pool(name="lists", bufs=1))
+        keep = ctx.enter_context(tc.tile_pool(name="keep", bufs=1))
+        ring = ctx.enter_context(tc.tile_pool(name="ring", bufs=4))
+        psum = ctx.enter_context(tc.psum_pool(name="psum", bufs=1))
+        psum2 = ctx.enter_context(tc.psum_pool(name="psum2", bufs=2))
+
+        def held(name, shape, dtype, tag=None):
+            return keep.tile(shape, dtype, name=name, tag=tag or name, align_bytes=64)
+
+        offs_t = lists.tile([P, S // LIST_ROWS], U16, name="offs_t")
+        kidx_t = lists.tile([P, H // LIST_ROWS], U16, name="kidx_t")
+        nb_t = lists.tile([P, S // LIST_ROWS], U16, name="nb_t")
+
+        xs_win = held("xs_win", [P, T], U8)
+        ds_win = held("ds_win", [P, G], U8)
+        nc.vector.memset(ds_win[:].bitcast(I32), 0)
+        nc.vector.memset(xs_win[:].bitcast(I32), 0)
+        warm = held("warm", [P, 8], F32)
+        nc.vector.memset(warm[:, 0:1], 0.0)
+
+        nc.sync.dma_start(kidx_t[:], kidx)
+        nc.sync.dma_start(offs_t[:], offs)
+        nc.scalar.dma_start(ds_win[0:P:8, :].bitcast(I32), d_scales[0].bitcast(I32))
+        for q in range(4):
+            (nc.gpsimd if q else nc.scalar).dma_start(xs_win[32 * q : 32 * q + 4, :].bitcast(I32), x_scales[0, 4 * q : 4 * q + 4, :].bitcast(I32))
+        nc.scalar.activation(warm[:, 4:5], warm[:, 0:1], ACT.Sigmoid)
+        w1_view = w1.rearrange("(p j) c -> p j c", j=PACK)
+        w1_raw = []
+        for h in range(2):
+            raw = held("w1_raw%d" % h, [P, PACK, H // 2], F32)
+            nc.sync.dma_start(raw[:], w1_view[:, :, h * (H // 2) : (h + 1) * (H // 2)])
+            w1_raw.append(raw)
+        xw_win = held("xw_win", [P, T], U32)
+        nc.sync.dma_start(xw_win[:].bitcast(I32), x_words[0].rearrange("p n t -> p (n t)").bitcast(I32))
+        nc.sync.dma_start(nb_t[:], nb)
+        gs_t = held("gs_t", [P, PACK], F32)
+        gn_t = held("gn_t", [P, PACK], F32)
+        nc.gpsimd.dma_start(gs_t[:], gs.rearrange("(p t) o -> p (t o)", t=PACK))
+        nc.gpsimd.dma_start(gn_t[:], gn.rearrange("(p t) o -> p (t o)", t=PACK))
+
+        ds_g = held("ds_g", [P, H], U8)
+        nc.vector.tensor_copy(ds_g[:], ds_win[:].indirect(kidx_t[:]))
+        ds_d = held("ds_d", [P, H], U8)
+        nc.vector.tensor_copy(ds_d[:].rearrange("p (t m) -> p m t", t=PACK), ds_g[:].rearrange("p (m t) -> p m t", t=PACK))
+        ds_f = held("ds_f", [P, H], U8)
+        nc.vector.tensor_copy(ds_f[:].bitcast(I32), ds_d[:].bitcast(I32))
+        for e in range(1, 4):
+            nc.gpsimd.dma_start(ds_f[e:P:32, :].bitcast(I32), ds_d[8 * e : P : 32, :].bitcast(I32))
+
+        xs_g = held("xs_g", [P, S], U8, "ds_win")
+        nc.vector.tensor_copy(xs_g[:], xs_win[:].indirect(offs_t[:]))
+        w1_bf = held("w1_bf", [P, PACK, P, PACK], BF16)
+        for h in range(2):
+            nc.scalar.copy(
+                w1_bf[:, :, h * 64 : (h + 1) * 64, :].rearrange("p t m j -> p m t j"),
+                w1_raw[h][:].rearrange("p j (m t) -> p m t j", t=PACK),
+            )
+        dw_win = held("dw_win", [P, G], U32, "w1_raw0")
+        nc.sync.dma_start(dw_win[:].bitcast(I32), d_words[0].rearrange("p n t -> p (n t)").bitcast(I32))
+        w2_raw = held("w2_raw", [P, PACK, N], F32, "w1_raw1")
+        nc.sync.dma_start(w2_raw[:], w2.rearrange("(p j) c -> p j c", j=PACK))
+        w1_c = held("w1_c", [P, H], U32, "xs_win")
+        w1_s = held("w1_s", [P, H], U8)
+        nc.vector.quantize_mx(out=w1_c[:].bitcast(FP8X4), scales=w1_s[:], in_=w1_bf[:].rearrange("p t m j -> p (t m j)"))
+
+        xw_g = held("xw_g", [P, S], U32, "w1_bf")
+        nc.vector.tensor_copy(xw_g[:], xw_win[:].indirect(offs_t[:]))
+
+        res_t = held("res_t", [P, N // P, S], F32, "xw_win")
+        nc.sync.dma_start(res_t[:], res.rearrange("(t p) j -> p t j", p=P))
+        hy = held("hy", [P, PACK, S], F32)
+        hy_win = [held("hy_win%d" % t, [P, S], F32) for t in range(PACK)]
+        y_ps = [psum.tile([P, S], F32, name="y%d" % t) for t in range(PACK)]
+        for t in range(PACK):
+            cols = slice(t * P, (t + 1) * P)
+            nc.tensor.matmul_mx(out=y_ps[t][:], lhsT=w1_c[:, cols].bitcast(FP8X4), lhsT_scale=w1_s[:, cols], rhs=xw_g[:].bitcast(FP8X4), rhs_scale=xs_g[:], start=True, stop=True)
+            nc.scalar.activation(hy_win[t][:], y_ps[t][:], ACT.Copy, scale=gs_t[:, t : t + 1])
+        for lo in range(0, S, S // 2):
+            for t in range(PACK):
+                nc.scalar.activation(hy[:, t, lo : lo + S // 2], y_ps[t][:, lo : lo + S // 2], ACT.Copy, scale=gs_t[:, t : t + 1])
+
+        dw_g = held("dw_g", [P, H], U32)
+        nc.vector.tensor_copy(dw_g[:], dw_win[:].indirect(kidx_t[:]))
+        dw_d = held("dw_d", [P, H], U32)
+        nc.vector.tensor_copy(dw_d[:].rearrange("p (t m) -> p m t", t=PACK), dw_g[:].rearrange("p (m t) -> p m t", t=PACK))
+
+        w2_bf = held("w2_bf", [P, N, PACK], BF16)
+        for lo in range(0, N, P):
+            nc.scalar.copy(w2_bf[:, lo : lo + P, :].rearrange("p (c i) t -> p c t i", i=4), w2_raw[:, :, lo : lo + P].rearrange("p t (c i) -> p c t i", i=4))
+        w2_c = held("w2_c", [P, N], U32)
+        w2_s = held("w2_s", [P, N], U8)
+
+        hy_nb = {}
+
+        def fetch(lo, hi):
+            got = held("nb%d" % lo, [P, PACK, hi - lo], F32, "nb")
+            for t in range(PACK):
+                nc.vector.tensor_copy(got[:, t, :], hy_win[t][:].indirect(nb_t[:, lo // LIST_ROWS : hi // LIST_ROWS]))
+            for j in range(lo, hi, UNIT):
+                hy_nb[j // UNIT] = got[:, :, j - lo : j - lo + UNIT]
+
+        zq_bf, z2_bf, sig, o_ps = {}, {}, {}, {}
+
+        def subtract(u):
+            zq_bf[u] = ring.tile([P, UNIT, PACK], BF16, name="zq_bf", align_bytes=64)
+            nc.vector.tensor_tensor(
+                zq_bf[u][:].rearrange("p (c i) t -> p c t i", i=4),
+                hy[:, :, u * UNIT : (u + 1) * UNIT].rearrange("p t (c i) -> p c t i", i=4),
+                hy_nb[u].rearrange("p t (c i) -> p c t i", i=4),
+                ALU.subtract,
+            )
+
+        def score(u):
+            codes = ring.tile([P, UNIT], U32, name="zq_c", align_bytes=64)
+            scales = ring.tile([P, UNIT], U8, name="zq_s", align_bytes=64)
+            nc.vector.quantize_mx(out=codes[:].bitcast(FP8X4), scales=scales[:], in_=zq_bf[u][:].rearrange("p j t -> p (j t)"))
+            s_ps = psum2.tile([P, PACK, UNIT], F32, name="s_ps")
+            for t in range(PACK):
+                cols = slice(t * P, (t + 1) * P)
+                nc.tensor.matmul_mx(out=s_ps[:, t, :], lhsT=dw_d[:, cols].bitcast(FP8X4), lhsT_scale=ds_f[:, cols], rhs=codes[:].bitcast(FP8X4), rhs_scale=scales[:], start=True, stop=True)
+            sig[u] = ring.tile([P, UNIT, PACK], F32, name="sig", align_bytes=64)
+            nc.scalar.activation(sig[u][:], s_ps[:].rearrange("p t j -> p j t"), ACT.Sigmoid, scale=0.0625)
+
+        def weigh(u):
+            z2_bf[u] = ring.tile([P, UNIT, PACK], BF16, name="z2_bf", align_bytes=64)
+            nc.vector.tensor_tensor(z2_bf[u][:], sig[u][:], gn_t[:].unsqueeze(1).to_broadcast([P, UNIT, PACK]), ALU.mult)
+
+        def project(u):
+            codes = ring.tile([P, UNIT], U32, name="z2_c", align_bytes=64)
+            scales = ring.tile([P, UNIT], U8, name="z2_s", align_bytes=64)
+            nc.vector.quantize_mx(out=codes[:].bitcast(FP8X4), scales=scales[:], in_=z2_bf[u][:].rearrange("p j t -> p (j t)"))
+            o_ps[u] = psum2.tile([P, N // P, UNIT], F32, name="o_ps")
+            for t in range(N // P):
+                cols = slice(t * P, (t + 1) * P)
+                nc.tensor.matmul_mx(out=o_ps[u][:, t, :], lhsT=w2_c[:, cols].bitcast(FP8X4), lhsT_scale=w2_s[:, cols], rhs=codes[:].bitcast(FP8X4), rhs_scale=scales[:], start=True, stop=True)
+
+        out_view = out.rearrange("(t p) j -> p t j", p=P)
+
+        def finish(u):
+            cols = slice(u * UNIT, (u + 1) * UNIT)
+            o_sb = held("o_sb%d" % u, [P, N // P, UNIT], F32)
+            nc.vector.tensor_tensor(o_sb[:], o_ps[u][:], res_t[:, :, cols], ALU.add)
+            nc.sync.dma_start(out_view[:, :, cols], o_sb[:])
+
+        fetch(*GATHERS[0])
+        subtract(0)
+        subtract(1)
+        score(0)
+        score(1)
+        fetch(*GATHERS[1])
+        subtract(2)
+        subtract(3)
+        nc.vector.quantize_mx(out=w2_c[:].bitcast(FP8X4), scales=w2_s[:], in_=w2_bf[:].rearrange("p m t -> p (m t)"))
+        score(2)
+        score(3)
+        weigh(0)
+        weigh(1)
+        project(0)
+        project(1)
+        weigh(2)
+        finish(0)
+        project(2)
+        weigh(3)
+        finish(1)
+        project(3)
+        finish(2)
+        finish(3)

@@ -19,7 +19,8 @@ P = 128
 PACK = 4
 LIST_ROWS = 16
 UNIT = 128
-GATHERS = ((0, 256), (256, 512))
+ON_SCALAR = 2
+GATHERS = ((0, 256), (256, 384), (384, 512))
 
 
 def tile_picked_pqhop_sigmoid_p_kernel(tc, x_words, x_scales, w1, gs, d_words, d_scales, gn, res, w2, offs, nb, kidx, out):
@@ -29,7 +30,7 @@ def tile_picked_pqhop_sigmoid_p_kernel(tc, x_words, x_scales, w1, gs, d_words, d
         keep = ctx.enter_context(tc.tile_pool(name="keep", bufs=1))
         ring = ctx.enter_context(tc.tile_pool(name="ring", bufs=4))
         psum = ctx.enter_context(tc.psum_pool(name="psum", bufs=1))
-        psum2 = ctx.enter_context(tc.psum_pool(name="psum2", bufs=2))
+        psum2 = ctx.enter_context(tc.psum_pool(name="psum2", bufs=4))
 
         def held(name, shape, dtype, tag=None):
             return keep.tile(shape, dtype, name=name, tag=tag or name, align_bytes=64)
@@ -40,42 +41,40 @@ def tile_picked_pqhop_sigmoid_p_kernel(tc, x_words, x_scales, w1, gs, d_words, d
 
         xs_win = held("xs_win", [P, T], U8)
         ds_win = held("ds_win", [P, G], U8)
-        nc.vector.memset(ds_win[:].bitcast(I32), 0)
         nc.vector.memset(xs_win[:].bitcast(I32), 0)
+        nc.vector.memset(ds_win[:].bitcast(I32), 0)
         warm = held("warm", [P, 8], F32)
-        nc.vector.memset(warm[:, 0:1], 0.0)
+        nc.gpsimd.memset(warm[:, 0:1], 0.0)
 
-        nc.sync.dma_start(kidx_t[:], kidx)
-        nc.sync.dma_start(offs_t[:], offs)
-        nc.scalar.dma_start(ds_win[0:P:8, :].bitcast(I32), d_scales[0].bitcast(I32))
-        for q in range(4):
-            (nc.gpsimd if q else nc.scalar).dma_start(xs_win[32 * q : 32 * q + 4, :].bitcast(I32), x_scales[0, 4 * q : 4 * q + 4, :].bitcast(I32))
         nc.scalar.activation(warm[:, 4:5], warm[:, 0:1], ACT.Sigmoid)
-        w1_view = w1.rearrange("(p j) c -> p j c", j=PACK)
-        w1_raw = []
-        for h in range(2):
-            raw = held("w1_raw%d" % h, [P, PACK, H // 2], F32)
-            nc.sync.dma_start(raw[:], w1_view[:, :, h * (H // 2) : (h + 1) * (H // 2)])
-            w1_raw.append(raw)
-        xw_win = held("xw_win", [P, T], U32)
-        nc.sync.dma_start(xw_win[:].bitcast(I32), x_words[0].rearrange("p n t -> p (n t)").bitcast(I32))
+        nc.sync.dma_start(offs_t[:], offs)
+        nc.sync.dma_start(kidx_t[:], kidx)
         nc.sync.dma_start(nb_t[:], nb)
+        w1_view = w1.rearrange("(p j) c -> p j c", j=PACK)
+        w1_raw = [held("w1_raw%d" % h, [P, PACK, H // 2], F32) for h in range(2)]
+        nc.sync.dma_start(w1_raw[0][:], w1_view[:, :, : H // 2])
+        nc.sync.dma_start(xs_win[0:P:8, :].bitcast(I32), x_scales[0].bitcast(I32))
+        nc.sync.dma_start(w1_raw[1][:], w1_view[:, :, H // 2 :])
         gs_t = held("gs_t", [P, PACK], F32)
         gn_t = held("gn_t", [P, PACK], F32)
-        nc.gpsimd.dma_start(gs_t[:], gs.rearrange("(p t) o -> p (t o)", t=PACK))
-        nc.gpsimd.dma_start(gn_t[:], gn.rearrange("(p t) o -> p (t o)", t=PACK))
+        nc.sync.dma_start(gs_t[:], gs.rearrange("(p t) o -> p (t o)", t=PACK))
+        nc.sync.dma_start(gn_t[:], gn.rearrange("(p t) o -> p (t o)", t=PACK))
+        nc.sync.dma_start(ds_win[0:P:8, :].bitcast(I32), d_scales[0].bitcast(I32))
+        xw_win = held("xw_win", [P, T], U32)
+        nc.sync.dma_start(xw_win[:].bitcast(I32), x_words[0].rearrange("p n t -> p (n t)").bitcast(I32))
 
+        def place_rows(name, got):
+            plane = held(name, [P, got.shape[1]], U8)
+            nc.vector.tensor_copy(plane[:].bitcast(I32), got[:].bitcast(I32))
+            for e in range(1, 4):
+                nc.sync.dma_start(plane[e:P:32, :].bitcast(I32), got[8 * e : P : 32, :].bitcast(I32))
+            return plane
+
+        xs_g = held("xs_g", [P, S], U8)
+        nc.vector.tensor_copy(xs_g[:], xs_win[:].indirect(offs_t[:]))
+        xs_f = place_rows("xs_f", xs_g)
         ds_g = held("ds_g", [P, H], U8)
         nc.vector.tensor_copy(ds_g[:], ds_win[:].indirect(kidx_t[:]))
-        ds_d = held("ds_d", [P, H], U8)
-        nc.vector.tensor_copy(ds_d[:].rearrange("p (t m) -> p m t", t=PACK), ds_g[:].rearrange("p (m t) -> p m t", t=PACK))
-        ds_f = held("ds_f", [P, H], U8)
-        nc.vector.tensor_copy(ds_f[:].bitcast(I32), ds_d[:].bitcast(I32))
-        for e in range(1, 4):
-            nc.gpsimd.dma_start(ds_f[e:P:32, :].bitcast(I32), ds_d[8 * e : P : 32, :].bitcast(I32))
-
-        xs_g = held("xs_g", [P, S], U8, "ds_win")
-        nc.vector.tensor_copy(xs_g[:], xs_win[:].indirect(offs_t[:]))
         w1_bf = held("w1_bf", [P, PACK, P, PACK], BF16)
         for h in range(2):
             nc.scalar.copy(
@@ -84,36 +83,33 @@ def tile_picked_pqhop_sigmoid_p_kernel(tc, x_words, x_scales, w1, gs, d_words, d
             )
         dw_win = held("dw_win", [P, G], U32, "w1_raw0")
         nc.sync.dma_start(dw_win[:].bitcast(I32), d_words[0].rearrange("p n t -> p (n t)").bitcast(I32))
-        w2_raw = held("w2_raw", [P, PACK, N], F32, "w1_raw1")
-        nc.sync.dma_start(w2_raw[:], w2.rearrange("(p j) c -> p j c", j=PACK))
-        w1_c = held("w1_c", [P, H], U32, "xs_win")
+        w1_c = held("w1_c", [P, H], U32)
         w1_s = held("w1_s", [P, H], U8)
         nc.vector.quantize_mx(out=w1_c[:].bitcast(FP8X4), scales=w1_s[:], in_=w1_bf[:].rearrange("p t m j -> p (t m j)"))
 
-        xw_g = held("xw_g", [P, S], U32, "w1_bf")
+        xw_g = held("xw_g", [P, S], U32)
         nc.vector.tensor_copy(xw_g[:], xw_win[:].indirect(offs_t[:]))
 
-        res_t = held("res_t", [P, N // P, S], F32, "xw_win")
-        nc.sync.dma_start(res_t[:], res.rearrange("(t p) j -> p t j", p=P))
+        w2_raw = held("w2_raw", [P, PACK, N], F32, "w1_bf")
+        nc.sync.dma_start(w2_raw[:], w2.rearrange("(p j) c -> p j c", j=PACK))
+        ds_d = held("ds_d", [P, H], U8, "xw_win")
+        nc.vector.tensor_copy(ds_d[:].rearrange("p (t m) -> p m t", t=PACK), ds_g[:].rearrange("p (m t) -> p m t", t=PACK))
+        ds_f = place_rows("ds_f", ds_d)
         hy = held("hy", [P, PACK, S], F32)
         hy_win = [held("hy_win%d" % t, [P, S], F32) for t in range(PACK)]
-        y_ps = [psum.tile([P, S], F32, name="y%d" % t) for t in range(PACK)]
+        y_ps = [psum.tile([P, S], F32, name="y%d" % t, tag="y%d" % t) for t in range(PACK)]
         for t in range(PACK):
             cols = slice(t * P, (t + 1) * P)
-            nc.tensor.matmul_mx(out=y_ps[t][:], lhsT=w1_c[:, cols].bitcast(FP8X4), lhsT_scale=w1_s[:, cols], rhs=xw_g[:].bitcast(FP8X4), rhs_scale=xs_g[:], start=True, stop=True)
+            nc.tensor.matmul_mx(out=y_ps[t][:], lhsT=w1_c[:, cols].bitcast(FP8X4), lhsT_scale=w1_s[:, cols], rhs=xw_g[:].bitcast(FP8X4), rhs_scale=xs_f[:], start=True, stop=True)
             nc.scalar.activation(hy_win[t][:], y_ps[t][:], ACT.Copy, scale=gs_t[:, t : t + 1])
         for lo in range(0, S, S // 2):
             for t in range(PACK):
                 nc.scalar.activation(hy[:, t, lo : lo + S // 2], y_ps[t][:, lo : lo + S // 2], ACT.Copy, scale=gs_t[:, t : t + 1])
 
-        dw_g = held("dw_g", [P, H], U32)
-        nc.vector.tensor_copy(dw_g[:], dw_win[:].indirect(kidx_t[:]))
-        dw_d = held("dw_d", [P, H], U32)
-        nc.vector.tensor_copy(dw_d[:].rearrange("p (t m) -> p m t", t=PACK), dw_g[:].rearrange("p (m t) -> p m t", t=PACK))
-
         w2_bf = held("w2_bf", [P, N, PACK], BF16)
         for lo in range(0, N, P):
             nc.scalar.copy(w2_bf[:, lo : lo + P, :].rearrange("p (c i) t -> p c t i", i=4), w2_raw[:, :, lo : lo + P].rearrange("p t (c i) -> p c t i", i=4))
+        sig = held("sig", [P, S // UNIT, PACK, UNIT], F32, "w1_bf")
         w2_c = held("w2_c", [P, N], U32)
         w2_s = held("w2_s", [P, N], U8)
 
@@ -126,7 +122,7 @@ def tile_picked_pqhop_sigmoid_p_kernel(tc, x_words, x_scales, w1, gs, d_words, d
             for j in range(lo, hi, UNIT):
                 hy_nb[j // UNIT] = got[:, :, j - lo : j - lo + UNIT]
 
-        zq_bf, z2_bf, sig, o_ps = {}, {}, {}, {}
+        zq_bf, z2_bf, pairs, o_ps = {}, {}, {}, {}
 
         def subtract(u):
             zq_bf[u] = ring.tile([P, UNIT, PACK], BF16, name="zq_bf", align_bytes=64)
@@ -145,18 +141,29 @@ def tile_picked_pqhop_sigmoid_p_kernel(tc, x_words, x_scales, w1, gs, d_words, d
             for t in range(PACK):
                 cols = slice(t * P, (t + 1) * P)
                 nc.tensor.matmul_mx(out=s_ps[:, t, :], lhsT=dw_d[:, cols].bitcast(FP8X4), lhsT_scale=ds_f[:, cols], rhs=codes[:].bitcast(FP8X4), rhs_scale=scales[:], start=True, stop=True)
-            sig[u] = ring.tile([P, UNIT, PACK], F32, name="sig", align_bytes=64)
-            nc.scalar.activation(sig[u][:], s_ps[:].rearrange("p t j -> p j t"), ACT.Sigmoid, scale=0.0625)
+            if u >= ON_SCALAR:
+                nc.scalar.activation(sig[:, u].rearrange("p t j -> p (t j)").rearrange("p (j t) -> p j t", t=PACK), s_ps[:].rearrange("p t j -> p j t"), ACT.Sigmoid, scale=0.0625)
+                return
+            nc.scalar.activation(sig[:, u], s_ps[:], ACT.Sigmoid, scale=0.0625)
+            pairs[u] = ring.tile([P, 2, UNIT, 2], BF16, name="pairs", align_bytes=64)
+            for t in range(PACK):
+                nc.scalar.activation(pairs[u][:, t // 2, :, t % 2], sig[:, u, t, :], ACT.Copy, scale=gn_t[:, t : t + 1])
 
         def weigh(u):
             z2_bf[u] = ring.tile([P, UNIT, PACK], BF16, name="z2_bf", align_bytes=64)
-            nc.vector.tensor_tensor(z2_bf[u][:], sig[u][:], gn_t[:].unsqueeze(1).to_broadcast([P, UNIT, PACK]), ALU.mult)
+            if u >= ON_SCALAR:
+                nc.vector.tensor_tensor(z2_bf[u][:], sig[:, u].rearrange("p t j -> p (t j)").rearrange("p (j t) -> p j t", t=PACK), gn_t[:].unsqueeze(1).to_broadcast([P, UNIT, PACK]), ALU.mult)
+                return
+            nc.vector.tensor_copy(
+                z2_bf[u][:].rearrange("p j t -> p (j t)").bitcast(F32).rearrange("p (c i h) -> p c h i", i=4, h=2),
+                pairs[u][:].rearrange("p h j e -> p (h j e)").bitcast(F32).rearrange("p (h c i) -> p c h i", i=4, h=2),
+            )
 
         def project(u):
             codes = ring.tile([P, UNIT], U32, name="z2_c", align_bytes=64)
             scales = ring.tile([P, UNIT], U8, name="z2_s", align_bytes=64)
             nc.vector.quantize_mx(out=codes[:].bitcast(FP8X4), scales=scales[:], in_=z2_bf[u][:].rearrange("p j t -> p (j t)"))
-            o_ps[u] = psum2.tile([P, N // P, UNIT], F32, name="o_ps")
+            o_ps[u] = psum.tile([P, N // P, UNIT], F32, name="o_ps%d" % u, tag="y%d" % u)
             for t in range(N // P):
                 cols = slice(t * P, (t + 1) * P)
                 nc.tensor.matmul_mx(out=o_ps[u][:, t, :], lhsT=w2_c[:, cols].bitcast(FP8X4), lhsT_scale=w2_s[:, cols], rhs=codes[:].bitcast(FP8X4), rhs_scale=scales[:], start=True, stop=True)
@@ -170,25 +177,31 @@ def tile_picked_pqhop_sigmoid_p_kernel(tc, x_words, x_scales, w1, gs, d_words, d
             nc.sync.dma_start(out_view[:, :, cols], o_sb[:])
 
         fetch(*GATHERS[0])
+        dw_g = held("dw_g", [P, H], U32)
+        nc.vector.tensor_copy(dw_g[:], dw_win[:].indirect(kidx_t[:]))
+        res_t = held("res_t", [P, N // P, S], F32, "w1_raw0")
+        nc.sync.dma_start(res_t[:], res.rearrange("(t p) j -> p t j", p=P))
+        dw_d = held("dw_d", [P, H], U32)
+        nc.vector.tensor_copy(dw_d[:].rearrange("p (t m) -> p m t", t=PACK), dw_g[:].rearrange("p (m t) -> p m t", t=PACK))
+
         subtract(0)
         subtract(1)
         score(0)
         score(1)
         fetch(*GATHERS[1])
         subtract(2)
-        subtract(3)
-        nc.vector.quantize_mx(out=w2_c[:].bitcast(FP8X4), scales=w2_s[:], in_=w2_bf[:].rearrange("p m t -> p (m t)"))
         score(2)
+        fetch(*GATHERS[2])
+        subtract(3)
         score(3)
+        nc.vector.quantize_mx(out=w2_c[:].bitcast(FP8X4), scales=w2_s[:], in_=w2_bf[:].rearrange("p m t -> p (m t)"))
         weigh(0)
         weigh(1)
         project(0)
         project(1)
         weigh(2)
-        finish(0)
-        project(2)
         weigh(3)
-        finish(1)
+        project(2)
         project(3)
-        finish(2)
-        finish(3)
+        for u in range(4):
+            finish(u)

@@ -18,9 +18,8 @@ ACT = mybir.ActivationFunctionType
 P = 128
 PACK = 4
 LIST_ROWS = 16
-UNIT = 128
-ON_SCALAR = 2
-GATHERS = ((0, 256), (256, 384), (384, 512))
+HALF = S // 2
+QUARTER = S // 4
 
 
 def tile_picked_pqhop_sigmoid_p_kernel(tc, x_words, x_scales, w1, gs, d_words, d_scales, gn, res, w2, offs, nb, kidx, out):
@@ -28,9 +27,7 @@ def tile_picked_pqhop_sigmoid_p_kernel(tc, x_words, x_scales, w1, gs, d_words, d
     with ExitStack() as ctx:
         lists = ctx.enter_context(tc.tile_pool(name="lists", bufs=1))
         keep = ctx.enter_context(tc.tile_pool(name="keep", bufs=1))
-        ring = ctx.enter_context(tc.tile_pool(name="ring", bufs=4))
         psum = ctx.enter_context(tc.psum_pool(name="psum", bufs=1))
-        psum2 = ctx.enter_context(tc.psum_pool(name="psum2", bufs=4))
 
         def held(name, shape, dtype, tag=None):
             return keep.tile(shape, dtype, name=name, tag=tag or name, align_bytes=64)
@@ -47,21 +44,21 @@ def tile_picked_pqhop_sigmoid_p_kernel(tc, x_words, x_scales, w1, gs, d_words, d
         nc.gpsimd.memset(warm[:, 0:1], 0.0)
 
         nc.scalar.activation(warm[:, 4:5], warm[:, 0:1], ACT.Sigmoid)
-        nc.sync.dma_start(offs_t[:], offs)
-        nc.sync.dma_start(kidx_t[:], kidx)
-        nc.sync.dma_start(nb_t[:], nb)
         w1_view = w1.rearrange("(p j) c -> p j c", j=PACK)
         w1_raw = [held("w1_raw%d" % h, [P, PACK, H // 2], F32) for h in range(2)]
+        nc.sync.dma_start(offs_t[:], offs)
         nc.sync.dma_start(w1_raw[0][:], w1_view[:, :, : H // 2])
+        nc.sync.dma_start(kidx_t[:], kidx)
+        nc.sync.dma_start(nb_t[:], nb)
         nc.sync.dma_start(xs_win[0:P:8, :].bitcast(I32), x_scales[0].bitcast(I32))
         nc.sync.dma_start(w1_raw[1][:], w1_view[:, :, H // 2 :])
         gs_t = held("gs_t", [P, PACK], F32)
         gn_t = held("gn_t", [P, PACK], F32)
         nc.sync.dma_start(gs_t[:], gs.rearrange("(p t) o -> p (t o)", t=PACK))
-        nc.sync.dma_start(gn_t[:], gn.rearrange("(p t) o -> p (t o)", t=PACK))
         nc.sync.dma_start(ds_win[0:P:8, :].bitcast(I32), d_scales[0].bitcast(I32))
         xw_win = held("xw_win", [P, T], U32)
         nc.sync.dma_start(xw_win[:].bitcast(I32), x_words[0].rearrange("p n t -> p (n t)").bitcast(I32))
+        nc.gpsimd.dma_start(gn_t[:], gn.rearrange("(p t) o -> p (t o)", t=PACK))
 
         def place_rows(name, got):
             plane = held(name, [P, got.shape[1]], U8)
@@ -69,6 +66,17 @@ def tile_picked_pqhop_sigmoid_p_kernel(tc, x_words, x_scales, w1, gs, d_words, d
             for e in range(1, 4):
                 nc.sync.dma_start(plane[e:P:32, :].bitcast(I32), got[8 * e : P : 32, :].bitcast(I32))
             return plane
+
+        def quantise(name, values):
+            width = values.shape[1] // PACK
+            codes = held(name + "_codes", [P, width], U32)
+            scales = held(name + "_scales", [P, width], U8)
+            nc.vector.quantize_mx(out=codes[:].bitcast(FP8X4), scales=scales[:], in_=values)
+            return codes, scales
+
+        def product(acc, left, t, right):
+            cols = slice(t * P, (t + 1) * P)
+            nc.tensor.matmul_mx(out=acc, lhsT=left[0][:, cols].bitcast(FP8X4), lhsT_scale=left[1][:, cols], rhs=right[0][:].bitcast(FP8X4), rhs_scale=right[1][:], start=True, stop=True)
 
         xs_g = held("xs_g", [P, S], U8)
         nc.vector.tensor_copy(xs_g[:], xs_win[:].indirect(offs_t[:]))
@@ -81,127 +89,112 @@ def tile_picked_pqhop_sigmoid_p_kernel(tc, x_words, x_scales, w1, gs, d_words, d
                 w1_bf[:, :, h * 64 : (h + 1) * 64, :].rearrange("p t m j -> p m t j"),
                 w1_raw[h][:].rearrange("p j (m t) -> p m t j", t=PACK),
             )
-        dw_win = held("dw_win", [P, G], U32, "w1_raw0")
+        w2_raw = held("w2_raw", [P, PACK, N], F32, "w1_raw0")
+        nc.sync.dma_start(w2_raw[:], w2.rearrange("(p j) c -> p j c", j=PACK))
+        w1_q = quantise("w1", w1_bf[:].rearrange("p t m j -> p (t m j)"))
+        dw_win = held("dw_win", [P, G], U32, "w1_bf")
         nc.sync.dma_start(dw_win[:].bitcast(I32), d_words[0].rearrange("p n t -> p (n t)").bitcast(I32))
-        w1_c = held("w1_c", [P, H], U32)
-        w1_s = held("w1_s", [P, H], U8)
-        nc.vector.quantize_mx(out=w1_c[:].bitcast(FP8X4), scales=w1_s[:], in_=w1_bf[:].rearrange("p t m j -> p (t m j)"))
 
         xw_g = held("xw_g", [P, S], U32)
         nc.vector.tensor_copy(xw_g[:], xw_win[:].indirect(offs_t[:]))
-
-        w2_raw = held("w2_raw", [P, PACK, N], F32, "w1_bf")
-        nc.sync.dma_start(w2_raw[:], w2.rearrange("(p j) c -> p j c", j=PACK))
         ds_d = held("ds_d", [P, H], U8, "xw_win")
         nc.vector.tensor_copy(ds_d[:].rearrange("p (t m) -> p m t", t=PACK), ds_g[:].rearrange("p (m t) -> p m t", t=PACK))
         ds_f = place_rows("ds_f", ds_d)
-        hy = held("hy", [P, PACK, S], F32)
-        hy_win = [held("hy_win%d" % t, [P, S], F32) for t in range(PACK)]
-        y_ps = [psum.tile([P, S], F32, name="y%d" % t, tag="y%d" % t) for t in range(PACK)]
-        for t in range(PACK):
-            cols = slice(t * P, (t + 1) * P)
-            nc.tensor.matmul_mx(out=y_ps[t][:], lhsT=w1_c[:, cols].bitcast(FP8X4), lhsT_scale=w1_s[:, cols], rhs=xw_g[:].bitcast(FP8X4), rhs_scale=xs_f[:], start=True, stop=True)
-            nc.scalar.activation(hy_win[t][:], y_ps[t][:], ACT.Copy, scale=gs_t[:, t : t + 1])
-        for lo in range(0, S, S // 2):
-            for t in range(PACK):
-                nc.scalar.activation(hy[:, t, lo : lo + S // 2], y_ps[t][:, lo : lo + S // 2], ACT.Copy, scale=gs_t[:, t : t + 1])
 
+        y_ps = [psum.tile([P, S], F32, name="y%d" % t, tag="y%d" % t) for t in range(PACK)]
+        gy = [held("gy%d" % t, [P, S], F32) for t in range(PACK)]
+        for t in range(PACK):
+            product(y_ps[t][:], w1_q, t, (xw_g, xs_f))
+            nc.scalar.activation(gy[t][:], y_ps[t][:], ACT.Copy, scale=gs_t[:, t : t + 1])
+
+        gy_all = held("gy_all", [P, PACK, S], F32)
+        for lo in range(0, S, HALF):
+            for t in range(PACK):
+                nc.scalar.activation(gy_all[:, t, lo : lo + HALF], y_ps[t][:, lo : lo + HALF], ACT.Copy, scale=gs_t[:, t : t + 1])
         w2_bf = held("w2_bf", [P, N, PACK], BF16)
         for lo in range(0, N, P):
             nc.scalar.copy(w2_bf[:, lo : lo + P, :].rearrange("p (c i) t -> p c t i", i=4), w2_raw[:, :, lo : lo + P].rearrange("p t (c i) -> p c t i", i=4))
-        sig = held("sig", [P, S // UNIT, PACK, UNIT], F32, "w1_bf")
-        w2_c = held("w2_c", [P, N], U32)
-        w2_s = held("w2_s", [P, N], U8)
 
-        hy_nb = {}
-
-        def fetch(lo, hi):
-            got = held("nb%d" % lo, [P, PACK, hi - lo], F32, "nb")
+        def fetch(half):
+            got = held("gy_nb%d" % half, [P, PACK, HALF], F32, "fetched")
             for t in range(PACK):
-                nc.vector.tensor_copy(got[:, t, :], hy_win[t][:].indirect(nb_t[:, lo // LIST_ROWS : hi // LIST_ROWS]))
-            for j in range(lo, hi, UNIT):
-                hy_nb[j // UNIT] = got[:, :, j - lo : j - lo + UNIT]
+                nc.vector.tensor_copy(got[:, t, :], gy[t][:].indirect(nb_t[:, half * HALF // LIST_ROWS : (half + 1) * HALF // LIST_ROWS]))
+            return got
 
-        zq_bf, z2_bf, pairs, o_ps = {}, {}, {}, {}
-
-        def subtract(u):
-            zq_bf[u] = ring.tile([P, UNIT, PACK], BF16, name="zq_bf", align_bytes=64)
+        def subtract(lo, hi, got):
+            zq_bf = held("zq_bf%d" % lo, [P, hi - lo, PACK], BF16)
             nc.vector.tensor_tensor(
-                zq_bf[u][:].rearrange("p (c i) t -> p c t i", i=4),
-                hy[:, :, u * UNIT : (u + 1) * UNIT].rearrange("p t (c i) -> p c t i", i=4),
-                hy_nb[u].rearrange("p t (c i) -> p c t i", i=4),
+                zq_bf[:].rearrange("p (c i) t -> p c t i", i=4),
+                gy_all[:, :, lo:hi].rearrange("p t (c i) -> p c t i", i=4),
+                got.rearrange("p t (c i) -> p c t i", i=4),
                 ALU.subtract,
             )
+            return zq_bf[:].rearrange("p j t -> p (j t)")
 
-        def score(u):
-            codes = ring.tile([P, UNIT], U32, name="zq_c", align_bytes=64)
-            scales = ring.tile([P, UNIT], U8, name="zq_s", align_bytes=64)
-            nc.vector.quantize_mx(out=codes[:].bitcast(FP8X4), scales=scales[:], in_=zq_bf[u][:].rearrange("p j t -> p (j t)"))
-            s_ps = psum2.tile([P, PACK, UNIT], F32, name="s_ps")
-            for t in range(PACK):
-                cols = slice(t * P, (t + 1) * P)
-                nc.tensor.matmul_mx(out=s_ps[:, t, :], lhsT=dw_d[:, cols].bitcast(FP8X4), lhsT_scale=ds_f[:, cols], rhs=codes[:].bitcast(FP8X4), rhs_scale=scales[:], start=True, stop=True)
-            if u >= ON_SCALAR:
-                nc.scalar.activation(sig[:, u].rearrange("p t j -> p (t j)").rearrange("p (j t) -> p j t", t=PACK), s_ps[:].rearrange("p t j -> p j t"), ACT.Sigmoid, scale=0.0625)
-                return
-            nc.scalar.activation(sig[:, u], s_ps[:], ACT.Sigmoid, scale=0.0625)
-            pairs[u] = ring.tile([P, 2, UNIT, 2], BF16, name="pairs", align_bytes=64)
-            for t in range(PACK):
-                nc.scalar.activation(pairs[u][:, t // 2, :, t % 2], sig[:, u, t, :], ACT.Copy, scale=gn_t[:, t : t + 1])
-
-        def weigh(u):
-            z2_bf[u] = ring.tile([P, UNIT, PACK], BF16, name="z2_bf", align_bytes=64)
-            if u >= ON_SCALAR:
-                nc.vector.tensor_tensor(z2_bf[u][:], sig[:, u].rearrange("p t j -> p (t j)").rearrange("p (j t) -> p j t", t=PACK), gn_t[:].unsqueeze(1).to_broadcast([P, UNIT, PACK]), ALU.mult)
-                return
-            nc.vector.tensor_copy(
-                z2_bf[u][:].rearrange("p j t -> p (j t)").bitcast(F32).rearrange("p (c i h) -> p c h i", i=4, h=2),
-                pairs[u][:].rearrange("p h j e -> p (h j e)").bitcast(F32).rearrange("p (h c i) -> p c h i", i=4, h=2),
-            )
-
-        def project(u):
-            codes = ring.tile([P, UNIT], U32, name="z2_c", align_bytes=64)
-            scales = ring.tile([P, UNIT], U8, name="z2_s", align_bytes=64)
-            nc.vector.quantize_mx(out=codes[:].bitcast(FP8X4), scales=scales[:], in_=z2_bf[u][:].rearrange("p j t -> p (j t)"))
-            o_ps[u] = psum.tile([P, N // P, UNIT], F32, name="o_ps%d" % u, tag="y%d" % u)
-            for t in range(N // P):
-                cols = slice(t * P, (t + 1) * P)
-                nc.tensor.matmul_mx(out=o_ps[u][:, t, :], lhsT=w2_c[:, cols].bitcast(FP8X4), lhsT_scale=w2_s[:, cols], rhs=codes[:].bitcast(FP8X4), rhs_scale=scales[:], start=True, stop=True)
-
-        out_view = out.rearrange("(t p) j -> p t j", p=P)
-
-        def finish(u):
-            cols = slice(u * UNIT, (u + 1) * UNIT)
-            o_sb = held("o_sb%d" % u, [P, N // P, UNIT], F32)
-            nc.vector.tensor_tensor(o_sb[:], o_ps[u][:], res_t[:, :, cols], ALU.add)
-            nc.sync.dma_start(out_view[:, :, cols], o_sb[:])
-
-        fetch(*GATHERS[0])
+        got = fetch(0)
         dw_g = held("dw_g", [P, H], U32)
         nc.vector.tensor_copy(dw_g[:], dw_win[:].indirect(kidx_t[:]))
-        res_t = held("res_t", [P, N // P, S], F32, "w1_raw0")
+        res_t = held("res_t", [P, N // P, S], F32, "w1_bf")
         nc.sync.dma_start(res_t[:], res.rearrange("(t p) j -> p t j", p=P))
         dw_d = held("dw_d", [P, H], U32)
         nc.vector.tensor_copy(dw_d[:].rearrange("p (t m) -> p m t", t=PACK), dw_g[:].rearrange("p (m t) -> p m t", t=PACK))
+        keys = (dw_d, ds_f)
+        zq0 = quantise("zq0", subtract(0, HALF, got[:]))
+        sig = held("sig", [P, PACK * S], F32)
+        sig0 = sig[:, : PACK * HALF].rearrange("p (t j) -> p t j", t=PACK)
+        pairs = held("pairs", [P, 2, HALF, 2], BF16)
+        for h in range(2):
+            s_ps = psum.tile([P, 2, HALF], F32, name="s0%d" % h)
+            for e in range(2):
+                product(s_ps[:, e, :], keys, 2 * h + e, zq0)
+            nc.scalar.activation(sig0[:, 2 * h : 2 * h + 2, :], s_ps[:], ACT.Sigmoid, scale=0.0625)
+            for e in range(2):
+                nc.scalar.activation(pairs[:, h, :, e], sig0[:, 2 * h + e, :], ACT.Copy, scale=gn_t[:, 2 * h + e : 2 * h + e + 1])
 
-        subtract(0)
-        subtract(1)
-        score(0)
-        score(1)
-        fetch(*GATHERS[1])
-        subtract(2)
-        score(2)
-        fetch(*GATHERS[2])
-        subtract(3)
-        score(3)
-        nc.vector.quantize_mx(out=w2_c[:].bitcast(FP8X4), scales=w2_s[:], in_=w2_bf[:].rearrange("p m t -> p (m t)"))
-        weigh(0)
-        weigh(1)
-        project(0)
-        project(1)
-        weigh(2)
-        weigh(3)
-        project(2)
-        project(3)
-        for u in range(4):
-            finish(u)
+        def score(lo, zq_bf):
+            zq = quantise("zq%d" % lo, zq_bf)
+            s_ps = psum.tile([P, PACK, QUARTER], F32, name="s%d" % lo)
+            for t in range(PACK):
+                product(s_ps[:, t, :], keys, t, zq)
+            part = sig[:, PACK * lo : PACK * (lo + QUARTER)].rearrange("p (j t) -> p j t", t=PACK)
+            nc.scalar.activation(part, s_ps[:].rearrange("p t j -> p j t"), ACT.Sigmoid, scale=0.0625)
+            return part
+
+        got = fetch(1)
+        zq_bf2 = subtract(HALF, HALF + QUARTER, got[:, :, :QUARTER])
+        zq_bf3 = subtract(HALF + QUARTER, S, got[:, :, QUARTER:])
+        sig2 = score(HALF, zq_bf2)
+        sig3 = score(HALF + QUARTER, zq_bf3)
+        w2_q = quantise("w2", w2_bf[:].rearrange("p m t -> p (m t)"))
+
+        z2_bf = [held("z2_bf%d" % h, [P, HALF, PACK], BF16) for h in range(2)]
+        nc.vector.tensor_copy(
+            z2_bf[0][:].rearrange("p j t -> p (j t)").bitcast(F32).rearrange("p (c i h) -> p c h i", i=4, h=2),
+            pairs[:].rearrange("p h j e -> p (h j e)").bitcast(F32).rearrange("p (h c i) -> p c h i", i=4, h=2),
+        )
+        out_view = out.rearrange("(t p) j -> p t j", p=P)
+
+        def project(h):
+            z2 = quantise("z2%d" % h, z2_bf[h][:].rearrange("p j t -> p (j t)"))
+            banks = []
+            for b in range(2):
+                o_ps = psum.tile([P, 2, HALF], F32, name="o%d%d" % (h, b), tag="y%d" % (2 * h + b))
+                for e in range(2):
+                    product(o_ps[:, e, :], w2_q, 2 * b + e, z2)
+                banks.append(o_ps)
+            return banks
+
+        def finish(h, banks):
+            cols = slice(h * HALF, (h + 1) * HALF)
+            for b in range(2):
+                o_sb = held("o_sb%d%d" % (h, b), [P, 2, HALF], F32)
+                nc.vector.tensor_tensor(o_sb[:], banks[b][:], res_t[:, 2 * b : 2 * b + 2, cols], ALU.add)
+                nc.sync.dma_start(out_view[:, 2 * b : 2 * b + 2, cols], o_sb[:])
+
+        gn_wide = gn_t[:].unsqueeze(1).to_broadcast([P, QUARTER, PACK])
+        first = project(0)
+        nc.vector.tensor_tensor(z2_bf[1][:, :QUARTER, :], sig2, gn_wide, ALU.mult)
+        nc.vector.tensor_tensor(z2_bf[1][:, QUARTER:, :], sig3, gn_wide, ALU.mult)
+        second = project(1)
+        finish(0, first)
+        finish(1, second)

from contextlib import ExitStack

import concourse.mybir as mybir

K, T, S, N, H, G = 512, 2048, 512, 512, 512, 2048
FLOPS = 2 * S * (K * H + K * H + H * N)

F32 = mybir.dt.float32
BF16 = mybir.dt.bfloat16
I32 = mybir.dt.int32
U32 = mybir.dt.uint32
U16 = mybir.dt.uint16
U8 = mybir.dt.uint8
FP8X4 = mybir.dt.float8_e4m3fn_x4
ALU = mybir.AluOpType
ACT = mybir.ActivationFunctionType

P = 128
PACK = 4
LIST_ROWS = 16
HALF = S // 2
QUARTER = S // 4


def tile_picked_pqhop_sigmoid_p_kernel(tc, x_words, x_scales, w1, gs, d_words, d_scales, gn, res, w2, offs, nb, kidx, out):
    nc = tc.nc
    with ExitStack() as ctx:
        lists = ctx.enter_context(tc.tile_pool(name="lists", bufs=1))
        keep = ctx.enter_context(tc.tile_pool(name="keep", bufs=1))
        psum = ctx.enter_context(tc.psum_pool(name="psum", bufs=1))

        def held(name, shape, dtype, tag=None):
            return keep.tile(shape, dtype, name=name, tag=tag or name, align_bytes=64)

        offs_t = lists.tile([P, S // LIST_ROWS], U16, name="offs_t")
        kidx_t = lists.tile([P, H // LIST_ROWS], U16, name="kidx_t")
        nb_t = lists.tile([P, S // LIST_ROWS], U16, name="nb_t")

        xs_win = held("xs_win", [P, T], U8)
        ds_win = held("ds_win", [P, G], U8)
        nc.vector.memset(xs_win[:].bitcast(I32), 0)
        nc.vector.memset(ds_win[:].bitcast(I32), 0)
        warm = held("warm", [P, 8], F32)
        nc.gpsimd.memset(warm[:, 0:1], 0.0)

        nc.scalar.activation(warm[:, 4:5], warm[:, 0:1], ACT.Sigmoid)
        w1_view = w1.rearrange("(p j) c -> p j c", j=PACK)
        w1_raw = [held("w1_raw%d" % h, [P, PACK, H // 2], F32) for h in range(2)]
        nc.sync.dma_start(offs_t[:], offs)
        nc.sync.dma_start(w1_raw[0][:], w1_view[:, :, : H // 2])
        nc.sync.dma_start(kidx_t[:], kidx)
        nc.sync.dma_start(nb_t[:], nb)
        nc.sync.dma_start(xs_win[0:P:8, :].bitcast(I32), x_scales[0].bitcast(I32))
        nc.sync.dma_start(w1_raw[1][:], w1_view[:, :, H // 2 :])
        gs_t = held("gs_t", [P, PACK], F32)
        gn_t = held("gn_t", [P, PACK], F32)
        nc.sync.dma_start(gs_t[:], gs.rearrange("(p t) o -> p (t o)", t=PACK))
        nc.sync.dma_start(ds_win[0:P:8, :].bitcast(I32), d_scales[0].bitcast(I32))
        xw_win = held("xw_win", [P, T], U32)
        nc.sync.dma_start(xw_win[:].bitcast(I32), x_words[0].rearrange("p n t -> p (n t)").bitcast(I32))
        nc.gpsimd.dma_start(gn_t[:], gn.rearrange("(p t) o -> p (t o)", t=PACK))

        def place_rows(name, got):
            plane = held(name, [P, got.shape[1]], U8)
            nc.vector.tensor_copy(plane[:].bitcast(I32), got[:].bitcast(I32))
            for e in range(1, 4):
                nc.sync.dma_start(plane[e:P:32, :].bitcast(I32), got[8 * e : P : 32, :].bitcast(I32))
            return plane

        def quantise(name, values):
            width = values.shape[1] // PACK
            codes = held(name + "_codes", [P, width], U32)
            scales = held(name + "_scales", [P, width], U8)
            nc.vector.quantize_mx(out=codes[:].bitcast(FP8X4), scales=scales[:], in_=values)
            return codes, scales

        def product(acc, left, t, right):
            cols = slice(t * P, (t + 1) * P)
            nc.tensor.matmul_mx(out=acc, lhsT=left[0][:, cols].bitcast(FP8X4), lhsT_scale=left[1][:, cols], rhs=right[0][:].bitcast(FP8X4), rhs_scale=right[1][:], start=True, stop=True)

        xs_g = held("xs_g", [P, S], U8)
        nc.vector.tensor_copy(xs_g[:], xs_win[:].indirect(offs_t[:]))
        xs_f = place_rows("xs_f", xs_g)
        ds_g = held("ds_g", [P, H], U8)
        nc.vector.tensor_copy(ds_g[:], ds_win[:].indirect(kidx_t[:]))
        w1_bf = held("w1_bf", [P, PACK, P, PACK], BF16)
        for h in range(2):
            nc.scalar.copy(
                w1_bf[:, :, h * 64 : (h + 1) * 64, :].rearrange("p t m j -> p m t j"),
                w1_raw[h][:].rearrange("p j (m t) -> p m t j", t=PACK),
            )
        w2_raw = held("w2_raw", [P, PACK, N], F32, "w1_raw0")
        nc.sync.dma_start(w2_raw[:], w2.rearrange("(p j) c -> p j c", j=PACK))
        w1_q = quantise("w1", w1_bf[:].rearrange("p t m j -> p (t m j)"))
        dw_win = held("dw_win", [P, G], U32, "w1_bf")
        nc.sync.dma_start(dw_win[:].bitcast(I32), d_words[0].rearrange("p n t -> p (n t)").bitcast(I32))

        xw_g = held("xw_g", [P, S], U32)
        nc.vector.tensor_copy(xw_g[:], xw_win[:].indirect(offs_t[:]))
        ds_d = held("ds_d", [P, H], U8, "xw_win")
        nc.vector.tensor_copy(ds_d[:].rearrange("p (t m) -> p m t", t=PACK), ds_g[:].rearrange("p (m t) -> p m t", t=PACK))
        ds_f = place_rows("ds_f", ds_d)

        y_ps = [psum.tile([P, S], F32, name="y%d" % t, tag="y%d" % t) for t in range(PACK)]
        gy = [held("gy%d" % t, [P, S], F32) for t in range(PACK)]
        for t in range(PACK):
            product(y_ps[t][:], w1_q, t, (xw_g, xs_f))
            nc.scalar.activation(gy[t][:], y_ps[t][:], ACT.Copy, scale=gs_t[:, t : t + 1])

        gy_all = held("gy_all", [P, PACK, S], F32)
        for lo in range(0, S, HALF):
            for t in range(PACK):
                nc.scalar.activation(gy_all[:, t, lo : lo + HALF], y_ps[t][:, lo : lo + HALF], ACT.Copy, scale=gs_t[:, t : t + 1])
        w2_bf = held("w2_bf", [P, N, PACK], BF16)
        for lo in range(0, N, P):
            nc.scalar.copy(w2_bf[:, lo : lo + P, :].rearrange("p (c i) t -> p c t i", i=4), w2_raw[:, :, lo : lo + P].rearrange("p t (c i) -> p c t i", i=4))

        def fetch(half):
            got = held("gy_nb%d" % half, [P, PACK, HALF], F32, "fetched")
            for t in range(PACK):
                nc.vector.tensor_copy(got[:, t, :], gy[t][:].indirect(nb_t[:, half * HALF // LIST_ROWS : (half + 1) * HALF // LIST_ROWS]))
            return got

        def subtract(lo, hi, got):
            zq_bf = held("zq_bf%d" % lo, [P, hi - lo, PACK], BF16)
            nc.vector.tensor_tensor(
                zq_bf[:].rearrange("p (c i) t -> p c t i", i=4),
                gy_all[:, :, lo:hi].rearrange("p t (c i) -> p c t i", i=4),
                got.rearrange("p t (c i) -> p c t i", i=4),
                ALU.subtract,
            )
            return zq_bf[:].rearrange("p j t -> p (j t)")

        got = fetch(0)
        dw_g = held("dw_g", [P, H], U32)
        nc.vector.tensor_copy(dw_g[:], dw_win[:].indirect(kidx_t[:]))
        res_t = held("res_t", [P, N // P, S], F32, "w1_bf")
        nc.sync.dma_start(res_t[:], res.rearrange("(t p) j -> p t j", p=P))
        dw_d = held("dw_d", [P, H], U32)
        nc.vector.tensor_copy(dw_d[:].rearrange("p (t m) -> p m t", t=PACK), dw_g[:].rearrange("p (m t) -> p m t", t=PACK))
        keys = (dw_d, ds_f)
        zq0 = quantise("zq0", subtract(0, HALF, got[:]))
        sig = held("sig", [P, PACK * S], F32)
        sig0 = sig[:, : PACK * HALF].rearrange("p (t j) -> p t j", t=PACK)
        pairs = held("pairs", [P, 2, HALF, 2], BF16)
        for h in range(2):
            s_ps = psum.tile([P, 2, HALF], F32, name="s0%d" % h)
            for e in range(2):
                product(s_ps[:, e, :], keys, 2 * h + e, zq0)
            nc.scalar.activation(sig0[:, 2 * h : 2 * h + 2, :], s_ps[:], ACT.Sigmoid, scale=0.0625)
            for e in range(2):
                nc.scalar.activation(pairs[:, h, :, e], sig0[:, 2 * h + e, :], ACT.Copy, scale=gn_t[:, 2 * h + e : 2 * h + e + 1])

        def score(lo, zq_bf):
            zq = quantise("zq%d" % lo, zq_bf)
            s_ps = psum.tile([P, PACK, QUARTER], F32, name="s%d" % lo)
            for t in range(PACK):
                product(s_ps[:, t, :], keys, t, zq)
            part = sig[:, PACK * lo : PACK * (lo + QUARTER)].rearrange("p (j t) -> p j t", t=PACK)
            nc.scalar.activation(part, s_ps[:].rearrange("p t j -> p j t"), ACT.Sigmoid, scale=0.0625)
            return part

        got = fetch(1)
        zq_bf2 = subtract(HALF, HALF + QUARTER, got[:, :, :QUARTER])
        zq_bf3 = subtract(HALF + QUARTER, S, got[:, :, QUARTER:])
        sig2 = score(HALF, zq_bf2)
        sig3 = score(HALF + QUARTER, zq_bf3)
        w2_q = quantise("w2", w2_bf[:].rearrange("p m t -> p (m t)"))

        z2_bf = [held("z2_bf%d" % h, [P, HALF, PACK], BF16) for h in range(2)]
        nc.vector.tensor_copy(
            z2_bf[0][:].rearrange("p j t -> p (j t)").bitcast(F32).rearrange("p (c i h) -> p c h i", i=4, h=2),
            pairs[:].rearrange("p h j e -> p (h j e)").bitcast(F32).rearrange("p (h c i) -> p c h i", i=4, h=2),
        )
        out_view = out.rearrange("(t p) j -> p t j", p=P)

        def project(h):
            z2 = quantise("z2%d" % h, z2_bf[h][:].rearrange("p j t -> p (j t)"))
            banks = []
            for b in range(2):
                o_ps = psum.tile([P, 2, HALF], F32, name="o%d%d" % (h, b), tag="y%d" % (2 * h + b))
                for e in range(2):
                    product(o_ps[:, e, :], w2_q, 2 * b + e, z2)
                banks.append(o_ps)
            return banks

        def finish(h, banks):
            cols = slice(h * HALF, (h + 1) * HALF)
            for b in range(2):
                o_sb = held("o_sb%d%d" % (h, b), [P, 2, HALF], F32)
                nc.vector.tensor_tensor(o_sb[:], banks[b][:], res_t[:, 2 * b : 2 * b + 2, cols], ALU.add)
                nc.sync.dma_start(out_view[:, 2 * b : 2 * b + 2, cols], o_sb[:])

        gn_wide = gn_t[:].unsqueeze(1).to_broadcast([P, QUARTER, PACK])
        first = project(0)
        nc.vector.tensor_tensor(z2_bf[1][:, :QUARTER, :], sig2, gn_wide, ALU.mult)
        nc.vector.tensor_tensor(z2_bf[1][:, QUARTER:, :], sig3, gn_wide, ALU.mult)
        second = project(1)
        finish(0, first)
        finish(1, second)
